import numpy as np
import ml_dtypes


def mxq(x, axis, fmt="e4m3"):
    dtype, down = {"e4m3": (ml_dtypes.float8_e4m3fn, 7), "e5m2": (ml_dtypes.float8_e5m2, 14)}[fmt]
    v = np.moveaxis(np.asarray(x, np.float32).astype(ml_dtypes.bfloat16).astype(np.float64), axis, -1)
    blocks = v.reshape(v.shape[:-1] + (-1, 32))
    amax = np.abs(blocks).max(-1, keepdims=True)
    byte = np.maximum(np.where(amax > 0, np.frexp(amax)[1] - 1 + 127, 0) - down, 1)
    scale = np.exp2(byte - 127.0)
    codes = (blocks / scale).astype(np.float32).astype(dtype).astype(np.float64)
    return np.moveaxis((codes * scale).reshape(v.shape), -1, axis)


WIDE = False


def mx_kscale(k):
    if not WIDE:
        return np.ones(k)
    levels = np.array([10, -10, 5, -5, 0])
    if k % 512:
        return np.exp2(np.random.permutation(np.resize(levels, k // 32))).repeat(32)
    a = np.empty((k // 512, 16))
    for p in range(k // 512):
        a[p, :8] = np.random.permutation(np.resize(levels, 8))
        for g in range(8):
            far = levels[np.abs(levels - a[p, g]) >= 10]
            a[p, g + 8] = far[np.random.randint(len(far))]
    return np.exp2(a.ravel()).repeat(32)


def f64(x):
    return np.asarray(x).astype(np.float64)


def striped(idx):
    return np.tile(idx.reshape(-1, 16).T, (8, 1)).astype(np.uint16)


def unstriped(offs):
    return offs[:16].T.reshape(-1).astype(np.int64)


E2M1 = np.array([0.0, 0.5, 1.0, 1.5, 2.0, 3.0, 4.0, 6.0, -0.0, -0.5, -1.0, -1.5, -2.0, -3.0, -4.0, -6.0])


def pack_weight(w, fmt):
    k, n = w.shape
    w = f64(np.asarray(w, np.float32).astype(ml_dtypes.bfloat16)).reshape(k // 32, 32, n)
    amax = np.abs(w).max(1)
    if fmt == "e4m3":
        byte = np.frexp(amax)[1] - 1 + 127 - 7
    else:
        mant, ex = np.frexp(amax / 6.0)
        byte = np.where(mant > 0.5, ex, ex - 1) + 127
    byte = np.clip(np.where(amax > 0, byte, 1), 1, 254)
    scaled = (w * np.exp2(127.0 - byte)[:, None, :]).reshape(k, n).astype(np.float32)
    by_word = np.ascontiguousarray(scaled.reshape(k // 512, 128, 4, n).transpose(0, 1, 3, 2))
    if fmt == "e4m3":
        words = by_word.astype(ml_dtypes.float8_e4m3fn).view(np.uint8)
    else:
        c = by_word.astype(ml_dtypes.float4_e2m1fn).view(np.uint8) & 0xF
        words = (c[..., 0::2] | (c[..., 1::2] << 4)).reshape(k // 512, 128, 2 * n)
    return np.ascontiguousarray(words), np.ascontiguousarray(byte.astype(np.uint8).reshape(k // 512, 16, n))


def unpack_weight(words, scales, fmt):
    g, _, n = scales.shape
    words = np.ascontiguousarray(words).reshape(g, 128, n, -1)
    if fmt == "e4m3":
        vals = words.view(ml_dtypes.float8_e4m3fn).astype(np.float64)
    else:
        nib = np.empty((g, 128, n, 4), np.uint8)
        nib[..., 0::2] = words & 0xF
        nib[..., 1::2] = words >> 4
        vals = E2M1[nib]
    vals = vals * np.repeat(np.exp2(scales.astype(np.float64) - 127.0), 8, axis=1)[..., None]
    return vals.transpose(0, 1, 3, 2).reshape(g * 512, n)


def gelu(v):
    return 0.5 * v * (1.0 + np.tanh(np.sqrt(2.0 / np.pi) * (v + 0.044715 * v**3)))


K, T, S, P, P2, H = 512, 4096, 2048, 1024, 512, 1024

def setup_inputs():
    n = np.random.standard_normal
    s = mx_kscale(K)[:, None]
    u = mx_kscale(H)[:, None]
    tab_words, tab_scales = pack_weight(n((K, T)) * s, "e4m3")
    w1 = 1.3 * n((K, H)) / np.sqrt(K) / s * u.T
    w2 = 1.3 * n((K, H)) / np.sqrt(K) / s * u.T
    w2_words, w2_scales = pack_weight(w2, "e2m1")
    w3 = 1.4 * n((H, H)) / np.sqrt(H) / u
    sc = np.exp(0.2 * n(H)) / u[:, 0]
    return {"tab_words": tab_words, "tab_scales": tab_scales,
            "offs": striped(np.random.permutation(T)[:S]),
            "pos1": striped(np.random.permutation(S)[:P]),
            "pos2": striped(np.random.permutation(S)[:P]),
            "pos3": striped(np.random.permutation(P)[:P2]),
            "pos4": striped(np.random.permutation(S)[:P2]),
            "w1": w1.astype(np.float32),
            "w2_words": w2_words, "w2_scales": w2_scales,
            "w3": w3.astype(np.float32), "sc": sc.astype(np.float32)}

def reference(tab_words, tab_scales, offs, pos1, pos2, pos3, pos4, w1, w2_words, w2_scales, w3, sc):
    v = unpack_weight(tab_words, tab_scales, "e4m3")[:, unstriped(offs)]
    w1q = mxq(f64(w1), 0, "e4m3")
    w2q = unpack_weight(w2_words, w2_scales, "e2m1")
    h = np.minimum(w1q.T @ v, w2q.T @ v)
    a1 = np.abs(h[:, unstriped(pos1)] - h[:, unstriped(pos2)])
    b = f64(sc)[:, None] * h[:, unstriped(pos4)]
    a2 = a1[:, unstriped(pos3)] * np.tanh(b)
    a2q = mxq(a2, 0, "e4m3")
    w3q = mxq(f64(w3), 0, "e4m3")
    return (w3q.T @ a2q) + b

@@ -1,0 +1,241 @@
+from contextlib import ExitStack
+
+import concourse.mybir as mybir
+
+K, T, S, NP, NK, H = 512, 4096, 2048, 1024, 512, 1024
+FLOPS = 2 * (2 * K * H * S) + 2 * H * H * NK
+
+F32 = mybir.dt.float32
+BF16 = mybir.dt.bfloat16
+I32 = mybir.dt.int32
+U32 = mybir.dt.uint32
+U16 = mybir.dt.uint16
+U8 = mybir.dt.uint8
+FP8X4 = mybir.dt.float8_e4m3fn_x4
+FP4X4 = mybir.dt.float4_e2m1fn_x4
+ALU = mybir.AluOpType
+ACT = mybir.ActivationFunctionType
+
+P = 128
+PACK = 4
+PASS = P * PACK
+BANK = 512
+GROUPS = H // PASS
+SLICES = H // P
+HALF = NK // 2
+ROW0 = P - 16
+
+
+def tile_list_inquest_account_contrast_kernel(
+    tc, tab_words, tab_scales, offs, pos1, pos2, pos3, pos4, w1, w2_words, w2_scales, w3, sc, out
+):
+    nc = tc.nc
+    with ExitStack() as ctx:
+        keep = ctx.enter_context(tc.tile_pool(name="keep", bufs=1))
+        ring = ctx.enter_context(tc.tile_pool(name="ring", bufs=2))
+        psum = ctx.enter_context(tc.psum_pool(name="psum", bufs=4))
+
+        offs_t = keep.tile([P, S // 16], U16)
+        pos1_t = keep.tile([P, NP // 16], U16)
+        pos2_t = keep.tile([P, NP // 16], U16)
+        pos3_t = keep.tile([P, NK // 16], U16)
+        pos4_t = keep.tile([P, NK // 16], U16)
+        tab_w = keep.tile([P, T], I32, align_bytes=64)
+        tab_s = keep.tile([P, T // 4], I32, align_bytes=64)
+        v_s_rows = keep.tile([P, S], U8, align_bytes=64)
+        w2_s_rows = keep.tile([P, H], U8, align_bytes=64)
+        v_w = keep.tile([P, S], U32, align_bytes=64)
+        v_s = keep.tile([P, S], U8, align_bytes=64)
+        w2_raw_w = keep.tile([P, H], U16, align_bytes=64)
+        w2_raw_s = keep.tile([P, H // 4], I32, align_bytes=64)
+        w2_w = keep.tile([P, H], U16, align_bytes=64)
+        w2_s = keep.tile([P, H], U8, align_bytes=64)
+        w1_w = keep.tile([P, H], U32, align_bytes=64)
+        w1_s = keep.tile([P, H], U8, align_bytes=64)
+        w3_w = [keep.tile([P, H], U32, align_bytes=64, name=f"w3_w{g}") for g in range(GROUPS)]
+        w3_s = [keep.tile([P, H], U8, align_bytes=64, name=f"w3_s{g}") for g in range(GROUPS)]
+        a2_w = [keep.tile([P, NK], U32, align_bytes=64, name=f"a2_w{g}") for g in range(GROUPS)]
+        a2_s = [keep.tile([P, NK], U8, align_bytes=64, name=f"a2_s{g}") for g in range(GROUPS)]
+        sc_t = keep.tile([P, GROUPS, PACK], F32)
+        b_t = [keep.tile([P, PACK, NK], F32, name=f"b{g}") for g in range(GROUPS)]
+
+        def load_scale_rows(plane, rows):
+            nc.sync.dma_start(out=plane[ROW0:, :], in_=rows.bitcast(I32))
+            nc.vector.memset(plane[:96, :], 0)
+            nc.vector.memset(plane[96:ROW0, :], 0)
+
+        def place_scale_rows(plane, rows):
+            for q in range(4):
+                nc.sync.dma_start(
+                    out=plane[32 * q : 32 * q + 4, :].bitcast(I32),
+                    in_=rows[ROW0 + 4 * q : ROW0 + 4 * q + 4, :].bitcast(I32),
+                )
+
+        def load_weight(w, k0, c0):
+            raw = ring.tile([P, PACK, PASS], F32, name="w_raw", bufs=4)
+            nc.sync.dma_start(out=raw[:], in_=w[k0 : k0 + PASS, c0 : c0 + PASS].rearrange("(p j) c -> p j c", j=PACK))
+            return raw
+
+        def round_weight(raw):
+            grouped = ring.tile([P, PASS * PACK], BF16, name="w_grouped", align_bytes=64)
+            dst = grouped[:].rearrange("p (i m j) -> p m i j", i=PACK, j=PACK)
+            src = raw[:].rearrange("p j (m i) -> p m i j", i=PACK)
+            for m0 in range(0, P, P // 2):
+                nc.scalar.copy(out=dst[:, m0 : m0 + P // 2], in_=src[:, m0 : m0 + P // 2])
+            return grouped
+
+        def quantize_weight(grouped, words, scales, c0):
+            nc.vector.quantize_mx(
+                out=words[:, c0 : c0 + PASS].bitcast(FP8X4), scales=scales[:, c0 : c0 + PASS], in_=grouped[:]
+            )
+
+        def deal_columns(dst, src):
+            nc.vector.tensor_copy(
+                out=dst.rearrange("p (g i m) -> p g i m", g=GROUPS, i=PACK),
+                in_=src.rearrange("p (g m i) -> p g i m", g=GROUPS, i=PACK),
+            )
+
+        load_scale_rows(w2_raw_s, w2_scales[0])
+        nc.sync.dma_start(out=offs_t[:], in_=offs)
+        load_scale_rows(tab_s, tab_scales[0])
+        nc.sync.dma_start(out=w2_raw_w[:].bitcast(I32), in_=w2_words[0].bitcast(I32))
+        w1_raw = [load_weight(w1, 0, 0)]
+        nc.sync.dma_start(out=tab_w[:], in_=tab_words[0].rearrange("p t i -> p (t i)").bitcast(I32))
+
+        deal_columns(w2_s_rows[:], w2_raw_s[:].bitcast(U8))
+        place_scale_rows(w2_s, w2_s_rows)
+        nc.vector.tensor_copy(v_s_rows[:], tab_s[:].bitcast(U8).indirect(offs_t[:]))
+        place_scale_rows(v_s, v_s_rows)
+        deal_columns(w2_w[:], w2_raw_w[:])
+        quantize_weight(round_weight(w1_raw[0]), w1_w, w1_s, 0)
+        for c in range(S // BANK):
+            nc.vector.tensor_copy(
+                v_w[:, c * BANK : (c + 1) * BANK],
+                tab_w[:].bitcast(U32).indirect(offs_t[:, c * BANK // 16 : (c + 1) * BANK // 16]),
+            )
+
+        nc.sync.dma_start(out=pos1_t[:], in_=pos1)
+        nc.sync.dma_start(out=pos4_t[:], in_=pos4)
+        nc.sync.dma_start(out=pos2_t[:], in_=pos2)
+        nc.sync.dma_start(out=sc_t[:], in_=sc.rearrange("(g p i) -> p g i", p=P, i=PACK))
+        nc.sync.dma_start(out=pos3_t[:], in_=pos3)
+        w1_raw.append(load_weight(w1, 0, PASS))
+
+        h_t, a1_t, tanh_t, sums_t = {}, {}, {}, {}
+        tanh_late = [ring.tile([P, PACK, HALF], F32, name=f"tanh_late{half}", bufs=1) for half in range(2)]
+
+        def products(s):
+            rows = slice(s * P, (s + 1) * P)
+            sums_t[s] = []
+            for c in range(S // BANK):
+                cols = slice(c * BANK, (c + 1) * BANK)
+                bank1 = psum.tile([P, BANK], F32, name="bank1")
+                bank2 = psum.tile([P, BANK], F32, name="bank2")
+                for bank, lhs, lhs_s in (
+                    (bank1, w1_w[:, rows].bitcast(FP8X4), w1_s[:, rows]),
+                    (bank2, w2_w[:, rows].bitcast(FP4X4), w2_s[:, rows]),
+                ):
+                    nc.tensor.matmul_mx(
+                        out=bank[:], lhsT=lhs, lhsT_scale=lhs_s,
+                        rhs=v_w[:, cols].bitcast(FP8X4), rhs_scale=v_s[:, cols], start=True, stop=True,
+                    )
+                first = ring.tile([P, BANK], F32, name="first", bufs=8)
+                nc.scalar.copy(out=first[:], in_=bank1[:])
+                sums_t[s].append((first, bank2))
+
+        def minimum(s):
+            h = ring.tile([P, S], F32, name="h")
+            h_t[s] = h
+            for c, (first, bank2) in enumerate(sums_t[s]):
+                nc.vector.tensor_tensor(out=h[:, c * BANK : (c + 1) * BANK], in0=bank2[:], in1=first[:], op=ALU.min)
+
+        def look_up(s):
+            g, i = divmod(s, PACK)
+            h = h_t[s]
+            scale = sc_t[:, g, i : i + 1]
+            left = ring.tile([P, NP], F32, name="left", bufs=1)
+            nc.vector.tensor_copy(left[:], h[:].indirect(pos1_t[:]))
+            note = ring.tile([P, NK], F32, name="note")
+            nc.vector.tensor_copy(note[:], h[:].indirect(pos4_t[:]))
+            diff = ring.tile([P, NP], F32, name="diff")
+            nc.vector.tensor_tensor(diff[:], h[:].indirect(pos2_t[:]), left[:], ALU.subtract)
+            a1 = ring.tile([P, NP], F32, name="a1", bufs=PACK)
+            nc.scalar.activation(out=a1[:], in_=diff[:], func=ACT.Abs)
+            a1_t[s] = a1
+            if g == 0:
+                tanh_b = ring.tile([P, NK], F32, name="tanh_b")
+                nc.scalar.activation(out=tanh_b[:], in_=note[:], func=ACT.Tanh, scale=scale)
+                tanh_t[s] = tanh_b
+            else:
+                for half in range(2):
+                    nc.scalar.activation(
+                        out=tanh_late[half][:, i, :], in_=note[:, half * HALF : (half + 1) * HALF], func=ACT.Tanh, scale=scale
+                    )
+            nc.scalar.activation(out=b_t[g][:, i, :], in_=note[:], func=ACT.Copy, scale=scale)
+
+        def keep_pairs(s, a2, tanh_b, j0, n):
+            nc.vector.tensor_tensor(
+                a2[:, s % PACK, :], a1_t[s][:].indirect(pos3_t[:, j0 // 16 : (j0 + n) // 16]), tanh_b, ALU.mult
+            )
+
+        def round_a2(a2, n):
+            grouped = ring.tile([P, n, PACK], BF16, name="a2_grouped", align_bytes=64)
+            nc.scalar.copy(out=grouped[:], in_=a2[:].rearrange("p i j -> p j i"))
+            return grouped
+
+        def quantize_a2(grouped, g, j0, n):
+            nc.vector.quantize_mx(
+                out=a2_w[g][:, j0 : j0 + n].bitcast(FP8X4),
+                scales=a2_s[g][:, j0 : j0 + n],
+                in_=grouped[:].rearrange("p j i -> p (j i)"),
+            )
+
+        def second_stage(j0):
+            cols = slice(j0, j0 + HALF)
+            for pair in range(SLICES // 2):
+                g, i0 = divmod(2 * pair, PACK)
+                bank = psum.tile([P, 2, HALF], F32, name=("bank1", "bank2")[pair % 2])
+                for kg in range(GROUPS):
+                    for u in range(2):
+                        rows = slice((2 * pair + u) * P, (2 * pair + u + 1) * P)
+                        nc.tensor.matmul_mx(
+                            out=bank[:, u, :], lhsT=w3_w[kg][:, rows].bitcast(FP8X4), lhsT_scale=w3_s[kg][:, rows],
+                            rhs=a2_w[kg][:, cols].bitcast(FP8X4), rhs_scale=a2_s[kg][:, cols],
+                            start=(kg == 0 and u == 0), stop=(kg == GROUPS - 1 and u == 1),
+                        )
+                result = ring.tile([P, 2, HALF], F32, name="result", bufs=4)
+                nc.vector.tensor_tensor(out=result[:], in0=bank[:], in1=b_t[g][:, i0 : i0 + 2, cols], op=ALU.add)
+                nc.sync.dma_start(
+                    out=out[g * PASS : (g + 1) * PASS, cols].rearrange("(p i) j -> p i j", i=PACK)[:, i0 : i0 + 2, :],
+                    in_=result[:],
+                )
+
+        w3_parts = [(kg, c0) for kg in range(GROUPS) for c0 in range(0, H, PASS)]
+        a2_first = keep.tile([P, PACK, NK], F32)
+        products(0)
+        minimum(0)
+        for s in range(SLICES):
+            if s + 1 < SLICES:
+                products(s + 1)
+            look_up(s)
+            if s == 0:
+                quantize_weight(round_weight(w1_raw[1]), w1_w, w1_s, PASS)
+            if s + 1 < SLICES:
+                minimum(s + 1)
+            if 1 <= s <= PACK:
+                keep_pairs(s - 1, a2_first, tanh_t[s - 1][:], 0, NK)
+            if 1 <= s < 1 + len(w3_parts):
+                kg, c0 = w3_parts[s - 1]
+                quantize_weight(round_weight(load_weight(w3, kg * PASS, c0)), w3_w[kg], w3_s[kg], c0)
+            if s == PACK + 1:
+                quantize_a2(round_a2(a2_first, NK), 0, 0, NK)
+
+        grouped_halves = []
+        for half, tag in enumerate(("left", "tanh_late0")):
+            a2_half = ring.tile([P, PACK, HALF], F32, name=tag, bufs=1)
+            for s in range(PACK, SLICES):
+                keep_pairs(s, a2_half, tanh_late[half][:, s % PACK, :], half * HALF, HALF)
+            grouped_halves.append(round_a2(a2_half, HALF))
+        for half in range(2):
+            quantize_a2(grouped_halves[half], 1, half * HALF, HALF)
+            second_stage(half * HALF)

@@ -1,6 +1,7 @@
 from contextlib import ExitStack
 
 import concourse.mybir as mybir
+from concourse.masks import make_identity
 
 K, T, S, NP, NK, H = 512, 4096, 2048, 1024, 512, 1024
 FLOPS = 2 * (2 * K * H * S) + 2 * H * H * NK
@@ -24,6 +25,7 @@ GROUPS = H // PASS
 SLICES = H // P
 HALF = NK // 2
 ROW0 = P - 16
+TURNED = (0, 1, 1, 1, 1, 1, 1, 2)
 
 
 def tile_list_inquest_account_contrast_kernel(
@@ -33,7 +35,7 @@ def tile_list_inquest_account_contrast_kernel(
     with ExitStack() as ctx:
         keep = ctx.enter_context(tc.tile_pool(name="keep", bufs=1))
         ring = ctx.enter_context(tc.tile_pool(name="ring", bufs=2))
-        psum = ctx.enter_context(tc.psum_pool(name="psum", bufs=4))
+        psum = ctx.enter_context(tc.psum_pool(name="psum", bufs=1))
 
         offs_t = keep.tile([P, S // 16], U16)
         pos1_t = keep.tile([P, NP // 16], U16)
@@ -44,7 +46,6 @@ def tile_list_inquest_account_contrast_kernel(
         tab_s = keep.tile([P, T // 4], I32, align_bytes=64)
         v_s_rows = keep.tile([P, S], U8, align_bytes=64)
         w2_s_rows = keep.tile([P, H], U8, align_bytes=64)
-        v_w = keep.tile([P, S], U32, align_bytes=64)
         v_s = keep.tile([P, S], U8, align_bytes=64)
         w2_raw_w = keep.tile([P, H], U16, align_bytes=64)
         w2_raw_s = keep.tile([P, H // 4], I32, align_bytes=64)
@@ -56,7 +57,8 @@ def tile_list_inquest_account_contrast_kernel(
         w3_s = [keep.tile([P, H], U8, align_bytes=64, name=f"w3_s{g}") for g in range(GROUPS)]
         a2_w = [keep.tile([P, NK], U32, align_bytes=64, name=f"a2_w{g}") for g in range(GROUPS)]
         a2_s = [keep.tile([P, NK], U8, align_bytes=64, name=f"a2_s{g}") for g in range(GROUPS)]
-        sc_t = keep.tile([P, GROUPS, PACK], F32)
+        identity = keep.tile([P, P], F32)
+        make_identity(nc, identity[:])
         b_t = [keep.tile([P, PACK, NK], F32, name=f"b{g}") for g in range(GROUPS)]
 
         def load_scale_rows(plane, rows):
@@ -72,16 +74,21 @@ def tile_list_inquest_account_contrast_kernel(
                 )
 
         def load_weight(w, k0, c0):
-            raw = ring.tile([P, PACK, PASS], F32, name="w_raw", bufs=4)
-            nc.sync.dma_start(out=raw[:], in_=w[k0 : k0 + PASS, c0 : c0 + PASS].rearrange("(p j) c -> p j c", j=PACK))
-            return raw
+            halves = []
+            for c in range(c0, c0 + PASS, PASS // 2):
+                raw = ring.tile([P, PACK, PASS // 2], F32, name="w_raw", bufs=2)
+                nc.sync.dma_start(
+                    out=raw[:], in_=w[k0 : k0 + PASS, c : c + PASS // 2].rearrange("(p j) c -> p j c", j=PACK)
+                )
+                halves.append(raw)
+            return halves
 
-        def round_weight(raw):
-            grouped = ring.tile([P, PASS * PACK], BF16, name="w_grouped", align_bytes=64)
+        def round_weight(raw, sign, tag="w_grouped", bufs=2):
+            grouped = ring.tile([P, PASS * PACK], BF16, name=tag, bufs=bufs, align_bytes=64)
             dst = grouped[:].rearrange("p (i m j) -> p m i j", i=PACK, j=PACK)
-            src = raw[:].rearrange("p j (m i) -> p m i j", i=PACK)
-            for m0 in range(0, P, P // 2):
-                nc.scalar.copy(out=dst[:, m0 : m0 + P // 2], in_=src[:, m0 : m0 + P // 2])
+            for half, m0 in zip(raw, range(0, P, P // 2)):
+                src = half[:].rearrange("p j (m i) -> p m i j", i=PACK)
+                nc.scalar.activation(out=dst[:, m0 : m0 + P // 2], in_=src, func=ACT.Copy, scale=sign)
             return grouped
 
         def quantize_weight(grouped, words, scales, c0):
@@ -89,71 +96,102 @@ def tile_list_inquest_account_contrast_kernel(
                 out=words[:, c0 : c0 + PASS].bitcast(FP8X4), scales=scales[:, c0 : c0 + PASS], in_=grouped[:]
             )
 
-        def deal_columns(dst, src):
-            nc.vector.tensor_copy(
+        def deal_columns(copy, dst, src):
+            copy(
                 out=dst.rearrange("p (g i m) -> p g i m", g=GROUPS, i=PACK),
                 in_=src.rearrange("p (g m i) -> p g i m", g=GROUPS, i=PACK),
             )
 
-        load_scale_rows(w2_raw_s, w2_scales[0])
         nc.sync.dma_start(out=offs_t[:], in_=offs)
         load_scale_rows(tab_s, tab_scales[0])
-        nc.sync.dma_start(out=w2_raw_w[:].bitcast(I32), in_=w2_words[0].bitcast(I32))
-        w1_raw = [load_weight(w1, 0, 0)]
+        load_scale_rows(w2_raw_s, w2_scales[0])
         nc.sync.dma_start(out=tab_w[:], in_=tab_words[0].rearrange("p t i -> p (t i)").bitcast(I32))
-
-        deal_columns(w2_s_rows[:], w2_raw_s[:].bitcast(U8))
-        place_scale_rows(w2_s, w2_s_rows)
-        nc.vector.tensor_copy(v_s_rows[:], tab_s[:].bitcast(U8).indirect(offs_t[:]))
-        place_scale_rows(v_s, v_s_rows)
-        deal_columns(w2_w[:], w2_raw_w[:])
-        quantize_weight(round_weight(w1_raw[0]), w1_w, w1_s, 0)
-        for c in range(S // BANK):
-            nc.vector.tensor_copy(
-                v_w[:, c * BANK : (c + 1) * BANK],
-                tab_w[:].bitcast(U32).indirect(offs_t[:, c * BANK // 16 : (c + 1) * BANK // 16]),
-            )
-
         nc.sync.dma_start(out=pos1_t[:], in_=pos1)
         nc.sync.dma_start(out=pos4_t[:], in_=pos4)
         nc.sync.dma_start(out=pos2_t[:], in_=pos2)
-        nc.sync.dma_start(out=sc_t[:], in_=sc.rearrange("(g p i) -> p g i", p=P, i=PACK))
         nc.sync.dma_start(out=pos3_t[:], in_=pos3)
+        w1_raw = [load_weight(w1, 0, 0)]
+        nc.sync.dma_start(out=w2_raw_w[:].bitcast(I32), in_=w2_words[0].bitcast(I32))
+
+        nc.vector.tensor_copy(v_s_rows[:], tab_s[:].bitcast(U8).indirect(offs_t[:]))
+        place_scale_rows(v_s, v_s_rows)
+        deal_columns(nc.vector.tensor_copy, w2_s_rows[:], w2_raw_s[:].bitcast(U8))
+        place_scale_rows(w2_s, w2_s_rows)
+        sc_t = keep.tile([P, GROUPS, PACK], F32, name="w2_raw_s", align_bytes=64)
+        nc.sync.dma_start(out=sc_t[:], in_=sc.rearrange("(g p i) -> p g i", p=P, i=PACK))
+        quantize_weight(round_weight(w1_raw[0], -1.0, "w1_first", 1), w1_w, w1_s, 0)
+        deal_columns(nc.scalar.copy, w2_w[:], w2_raw_w[:])
+        v_w = []
+        for c in range(S // BANK):
+            tag = "w1_first" if c == S // BANK - 1 else f"v_w{c}"
+            words = ring.tile([P, BANK], U32, name=tag, bufs=1, align_bytes=64)
+            nc.vector.tensor_copy(
+                words[:], tab_w[:].bitcast(U32).indirect(offs_t[:, c * BANK // 16 : (c + 1) * BANK // 16])
+            )
+            v_w.append(words)
         w1_raw.append(load_weight(w1, 0, PASS))
 
         h_t, a1_t, tanh_t, sums_t = {}, {}, {}, {}
-        tanh_late = [ring.tile([P, PACK, HALF], F32, name=f"tanh_late{half}", bufs=1) for half in range(2)]
+        tanh_late = [ring.tile([P, PACK, HALF], F32, name=f"tanh_late{half}", bufs=1, align_bytes=64) for half in range(2)]
 
         def products(s):
             rows = slice(s * P, (s + 1) * P)
+            w1_slice = (w1_w[:, rows].bitcast(FP8X4), w1_s[:, rows])
+            w2_slice = (w2_w[:, rows].bitcast(FP4X4), w2_s[:, rows])
+            h = ring.tile([P, S], F32, name="h", bufs=3)
+            h_t[s] = h
+
+            for c in range(TURNED[s]):
+                minus_first = psum.tile([P, PACK, P], F32, name="minus_first")
+                gap = psum.tile([P, PACK, P], F32, name="gap")
+                for bank, weights in ((minus_first, (w1_slice,)), (gap, (w1_slice, w2_slice))):
+                    for block in range(PACK):
+                        cols = slice(c * BANK + block * P, c * BANK + (block + 1) * P)
+                        for n, (words, scales) in enumerate(weights):
+                            nc.tensor.matmul_mx(
+                                out=bank[:, block, :], lhsT=v_w[c][:, block * P : (block + 1) * P].bitcast(FP8X4), lhsT_scale=v_s[:, cols],
+                                rhs=words, rhs_scale=scales, start=(n == 0), stop=(n == len(weights) - 1),
+                            )
+                terms = [ring.tile([P, PACK, P], F32, name=f"term{n}") for n in range(2)]
+                nc.scalar.copy(out=terms[0][:], in_=minus_first[:])
+                nc.scalar.activation(out=terms[1][:], in_=gap[:], func=ACT.Relu, scale=-1.0)
+                turned = psum.tile([P, PACK, P], F32, name="turned")
+                for block in range(PACK):
+                    for n, term in enumerate(terms):
+                        nc.tensor.matmul(
+                            out=turned[:, block, :], lhsT=term[:, block, :], rhs=identity[:],
+                            is_transpose=True, start=(n == 0), stop=(n == 1),
+                        )
+                nc.scalar.activation(
+                    out=h[:, c * BANK : (c + 1) * BANK], in_=turned[:].rearrange("p b j -> p (b j)"), func=ACT.Copy, scale=-1.0
+                )
+
             sums_t[s] = []
-            for c in range(S // BANK):
+            for c in range(TURNED[s], S // BANK):
                 cols = slice(c * BANK, (c + 1) * BANK)
-                bank1 = psum.tile([P, BANK], F32, name="bank1")
-                bank2 = psum.tile([P, BANK], F32, name="bank2")
-                for bank, lhs, lhs_s in (
-                    (bank1, w1_w[:, rows].bitcast(FP8X4), w1_s[:, rows]),
-                    (bank2, w2_w[:, rows].bitcast(FP4X4), w2_s[:, rows]),
-                ):
-                    nc.tensor.matmul_mx(
-                        out=bank[:], lhsT=lhs, lhsT_scale=lhs_s,
-                        rhs=v_w[:, cols].bitcast(FP8X4), rhs_scale=v_s[:, cols], start=True, stop=True,
-                    )
-                first = ring.tile([P, BANK], F32, name="first", bufs=8)
-                nc.scalar.copy(out=first[:], in_=bank1[:])
-                sums_t[s].append((first, bank2))
+                bank1 = psum.tile([P, BANK], F32, name="bank1", bufs=2)
+                table_product(bank1, w1_slice, cols)
+                first = ring.tile([P, BANK], F32, name="first", bufs=9)
+                nc.scalar.activation(out=first[:], in_=bank1[:], func=ACT.Copy, scale=-1.0)
+                sums_t[s].append((cols, first, w2_slice))
+
+        def table_product(bank, weight, cols):
+            nc.tensor.matmul_mx(
+                out=bank[:], lhsT=weight[0], lhsT_scale=weight[1],
+                rhs=v_w[cols.start // BANK][:].bitcast(FP8X4), rhs_scale=v_s[:, cols], start=True, stop=True,
+            )
 
         def minimum(s):
-            h = ring.tile([P, S], F32, name="h")
-            h_t[s] = h
-            for c, (first, bank2) in enumerate(sums_t[s]):
-                nc.vector.tensor_tensor(out=h[:, c * BANK : (c + 1) * BANK], in0=bank2[:], in1=first[:], op=ALU.min)
+            for cols, first, w2_slice in sums_t[s]:
+                bank2 = psum.tile([P, BANK], F32, name="bank2", bufs=3)
+                table_product(bank2, w2_slice, cols)
+                nc.vector.tensor_tensor(out=h_t[s][:, cols], in0=bank2[:], in1=first[:], op=ALU.min)
 
         def look_up(s):
             g, i = divmod(s, PACK)
             h = h_t[s]
             scale = sc_t[:, g, i : i + 1]
-            left = ring.tile([P, NP], F32, name="left", bufs=1)
+            left = ring.tile([P, NP], F32, name="left", bufs=1, align_bytes=64)
             nc.vector.tensor_copy(left[:], h[:].indirect(pos1_t[:]))
             note = ring.tile([P, NK], F32, name="note")
             nc.vector.tensor_copy(note[:], h[:].indirect(pos4_t[:]))
@@ -178,23 +216,21 @@ def tile_list_inquest_account_contrast_kernel(
                 a2[:, s % PACK, :], a1_t[s][:].indirect(pos3_t[:, j0 // 16 : (j0 + n) // 16]), tanh_b, ALU.mult
             )
 
-        def round_a2(a2, n):
-            grouped = ring.tile([P, n, PACK], BF16, name="a2_grouped", align_bytes=64)
-            nc.scalar.copy(out=grouped[:], in_=a2[:].rearrange("p i j -> p j i"))
-            return grouped
+        def round_a2(a2, grouped):
+            nc.scalar.copy(out=grouped.rearrange("p (j i) -> p j i", i=PACK), in_=a2.rearrange("p i j -> p j i"))
 
         def quantize_a2(grouped, g, j0, n):
             nc.vector.quantize_mx(
                 out=a2_w[g][:, j0 : j0 + n].bitcast(FP8X4),
                 scales=a2_s[g][:, j0 : j0 + n],
-                in_=grouped[:].rearrange("p j i -> p (j i)"),
+                in_=grouped,
             )
 
-        def second_stage(j0):
+        def second_stage(j0, banks):
             cols = slice(j0, j0 + HALF)
             for pair in range(SLICES // 2):
                 g, i0 = divmod(2 * pair, PACK)
-                bank = psum.tile([P, 2, HALF], F32, name=("bank1", "bank2")[pair % 2])
+                bank = psum.tile([P, 2, HALF], F32, name=banks[pair][0], bufs=banks[pair][1])
                 for kg in range(GROUPS):
                     for u in range(2):
                         rows = slice((2 * pair + u) * P, (2 * pair + u + 1) * P)
@@ -214,28 +250,36 @@ def tile_list_inquest_account_contrast_kernel(
         a2_first = keep.tile([P, PACK, NK], F32)
         products(0)
         minimum(0)
+        products(1)
         for s in range(SLICES):
-            if s + 1 < SLICES:
-                products(s + 1)
+            if s + 2 < SLICES:
+                products(s + 2)
             look_up(s)
             if s == 0:
-                quantize_weight(round_weight(w1_raw[1]), w1_w, w1_s, PASS)
+                quantize_weight(round_weight(w1_raw[1], -1.0), w1_w, w1_s, PASS)
             if s + 1 < SLICES:
                 minimum(s + 1)
             if 1 <= s <= PACK:
                 keep_pairs(s - 1, a2_first, tanh_t[s - 1][:], 0, NK)
             if 1 <= s < 1 + len(w3_parts):
                 kg, c0 = w3_parts[s - 1]
-                quantize_weight(round_weight(load_weight(w3, kg * PASS, c0)), w3_w[kg], w3_s[kg], c0)
+                quantize_weight(round_weight(load_weight(w3, kg * PASS, c0), 1.0), w3_w[kg], w3_s[kg], c0)
             if s == PACK + 1:
-                quantize_a2(round_a2(a2_first, NK), 0, 0, NK)
+                grouped = ring.tile([P, NK * PACK], BF16, name="w_grouped", align_bytes=64)
+                round_a2(a2_first[:], grouped[:])
+                quantize_a2(grouped[:], 0, 0, NK)
 
-        grouped_halves = []
-        for half, tag in enumerate(("left", "tanh_late0")):
-            a2_half = ring.tile([P, PACK, HALF], F32, name=tag, bufs=1)
+        a2_halves = [
+            ring.tile([P, PACK * HALF], F32, name="left", bufs=1, align_bytes=64),
+            ring.tile([P, (PACK + 1) * HALF], F32, name="tanh_late0", bufs=1, align_bytes=64),
+        ]
+        grouped_last = ring.tile([P, HALF * PACK], BF16, name="w_grouped", align_bytes=64)
+        grouped_halves = [a2_halves[1][:, (PACK - 1) * HALF :].bitcast(BF16), grouped_last[:]]
+        for half in range(2):
+            a2_half = a2_halves[half][:, : PACK * HALF].rearrange("p (i j) -> p i j", i=PACK)
             for s in range(PACK, SLICES):
                 keep_pairs(s, a2_half, tanh_late[half][:, s % PACK, :], half * HALF, HALF)
-            grouped_halves.append(round_a2(a2_half, HALF))
-        for half in range(2):
+            round_a2(a2_half, grouped_halves[half])
             quantize_a2(grouped_halves[half], 1, half * HALF, HALF)
-            second_stage(half * HALF)
+        second_stage(0, (("minus_first", 1), ("gap", 1), ("turned", 1), ("bank1", 2)))
+        second_stage(HALF, (("bank1", 2), ("bank2", 3), ("bank2", 3), ("bank2", 3)))

@@ -21,11 +21,19 @@ P = 128
 PACK = 4
 PASS = P * PACK
 BANK = 512
+TILES = S // BANK
+BLOCKS = BANK // P
 GROUPS = H // PASS
 SLICES = H // P
 HALF = NK // 2
-ROW0 = P - 16
-TURNED = (0, 1, 1, 1, 1, 1, 1, 2)
+PER_COLUMN = 16
+QUADRANTS, QUADRANT, SCALE_ROWS = 4, 32, 4
+ROW0 = P - QUADRANTS * SCALE_ROWS
+RUN = 4
+
+
+def turned_tiles(s):
+    return {0: 0, SLICES - 1: 2}.get(s, 1)
 
 
 def tile_list_inquest_account_contrast_kernel(
@@ -37,15 +45,14 @@ def tile_list_inquest_account_contrast_kernel(
         ring = ctx.enter_context(tc.tile_pool(name="ring", bufs=2))
         psum = ctx.enter_context(tc.psum_pool(name="psum", bufs=1))
 
-        offs_t = keep.tile([P, S // 16], U16)
-        pos1_t = keep.tile([P, NP // 16], U16)
-        pos2_t = keep.tile([P, NP // 16], U16)
-        pos3_t = keep.tile([P, NK // 16], U16)
-        pos4_t = keep.tile([P, NK // 16], U16)
+        offs_t = keep.tile([P, S // PER_COLUMN], U16)
+        pos1_t = keep.tile([P, NP // PER_COLUMN], U16)
+        pos2_t = keep.tile([P, NP // PER_COLUMN], U16)
+        pos3_t = keep.tile([P, NK // PER_COLUMN], U16)
+        pos4_t = keep.tile([P, NK // PER_COLUMN], U16)
         tab_w = keep.tile([P, T], I32, align_bytes=64)
         tab_s = keep.tile([P, T // 4], I32, align_bytes=64)
         v_s_rows = keep.tile([P, S], U8, align_bytes=64)
-        w2_s_rows = keep.tile([P, H], U8, align_bytes=64)
         v_s = keep.tile([P, S], U8, align_bytes=64)
         w2_raw_w = keep.tile([P, H], U16, align_bytes=64)
         w2_raw_s = keep.tile([P, H // 4], I32, align_bytes=64)
@@ -58,43 +65,31 @@ def tile_list_inquest_account_contrast_kernel(
         a2_w = [keep.tile([P, NK], U32, align_bytes=64, name=f"a2_w{g}") for g in range(GROUPS)]
         a2_s = [keep.tile([P, NK], U8, align_bytes=64, name=f"a2_s{g}") for g in range(GROUPS)]
         identity = keep.tile([P, P], F32)
-        make_identity(nc, identity[:])
         b_t = [keep.tile([P, PACK, NK], F32, name=f"b{g}") for g in range(GROUPS)]
 
-        def load_scale_rows(plane, rows):
-            nc.sync.dma_start(out=plane[ROW0:, :], in_=rows.bitcast(I32))
-            nc.vector.memset(plane[:96, :], 0)
-            nc.vector.memset(plane[96:ROW0, :], 0)
-
         def place_scale_rows(plane, rows):
-            for q in range(4):
+            for q in range(QUADRANTS):
                 nc.sync.dma_start(
-                    out=plane[32 * q : 32 * q + 4, :].bitcast(I32),
-                    in_=rows[ROW0 + 4 * q : ROW0 + 4 * q + 4, :].bitcast(I32),
+                    out=plane[QUADRANT * q : QUADRANT * q + SCALE_ROWS, :],
+                    in_=rows[SCALE_ROWS * q : SCALE_ROWS * (q + 1), :],
                 )
 
-        def load_weight(w, k0, c0):
-            halves = []
-            for c in range(c0, c0 + PASS, PASS // 2):
-                raw = ring.tile([P, PACK, PASS // 2], F32, name="w_raw", bufs=2)
-                nc.sync.dma_start(
-                    out=raw[:], in_=w[k0 : k0 + PASS, c : c + PASS // 2].rearrange("(p j) c -> p j c", j=PACK)
-                )
-                halves.append(raw)
-            return halves
+        def by_word(rows):
+            return rows.rearrange("(p j) c -> p j c", j=PACK)
 
-        def round_weight(raw, sign, tag="w_grouped", bufs=2):
+        def column_halves(raw, c0):
+            return [raw[:, :, c : c + PASS // 2] for c in range(c0, c0 + PASS, PASS // 2)]
+
+        def round_weight(halves, sign, tag="grouped", bufs=2):
             grouped = ring.tile([P, PASS * PACK], BF16, name=tag, bufs=bufs, align_bytes=64)
             dst = grouped[:].rearrange("p (i m j) -> p m i j", i=PACK, j=PACK)
-            for half, m0 in zip(raw, range(0, P, P // 2)):
-                src = half[:].rearrange("p j (m i) -> p m i j", i=PACK)
+            for half, m0 in zip(halves, range(0, P, P // 2)):
+                src = half.rearrange("p j (m i) -> p m i j", i=PACK)
                 nc.scalar.activation(out=dst[:, m0 : m0 + P // 2], in_=src, func=ACT.Copy, scale=sign)
-            return grouped
+            return grouped[:]
 
-        def quantize_weight(grouped, words, scales, c0):
-            nc.vector.quantize_mx(
-                out=words[:, c0 : c0 + PASS].bitcast(FP8X4), scales=scales[:, c0 : c0 + PASS], in_=grouped[:]
-            )
+        def quantize(grouped, words, plane, cols):
+            nc.vector.quantize_mx(out=words[:, cols].bitcast(FP8X4), scales=plane[:, cols], in_=grouped)
 
         def deal_columns(copy, dst, src):
             copy(
@@ -102,184 +97,202 @@ def tile_list_inquest_account_contrast_kernel(
                 in_=src.rearrange("p (g m i) -> p g i m", g=GROUPS, i=PACK),
             )
 
+        nc.gpsimd.memset(w2_raw_s[:], 0)
+        make_identity(nc, identity[:])
+        nc.vector.memset(tab_s[: P - QUADRANT, :], 0)
+        nc.vector.memset(tab_s[P - QUADRANT : ROW0, :], 0)
         nc.sync.dma_start(out=offs_t[:], in_=offs)
-        load_scale_rows(tab_s, tab_scales[0])
-        load_scale_rows(w2_raw_s, w2_scales[0])
+        nc.sync.dma_start(out=tab_s[ROW0:, :], in_=tab_scales[0].bitcast(I32))
         nc.sync.dma_start(out=tab_w[:], in_=tab_words[0].rearrange("p t i -> p (t i)").bitcast(I32))
+        place_scale_rows(w2_raw_s, w2_scales[0].bitcast(I32))
+        w1_early = []
+        for c in range(0, PASS, PASS // 2):
+            raw = ring.tile([P, PACK, PASS // 2], F32, name="w1_early")
+            nc.sync.dma_start(out=raw[:], in_=by_word(w1[:, c : c + PASS // 2]))
+            w1_early.append(raw[:])
+        nc.sync.dma_start(out=w2_raw_w[:].bitcast(I32), in_=w2_words[0].bitcast(I32))
+
+        nc.vector.tensor_copy(v_s_rows[:], tab_s[:].bitcast(U8).indirect(offs_t[:]))
+        place_scale_rows(v_s[:].bitcast(I32), v_s_rows[ROW0:, :].bitcast(I32))
+        deal_columns(nc.vector.tensor_copy, w2_s[:], w2_raw_s[:].bitcast(U8))
         nc.sync.dma_start(out=pos1_t[:], in_=pos1)
         nc.sync.dma_start(out=pos4_t[:], in_=pos4)
         nc.sync.dma_start(out=pos2_t[:], in_=pos2)
         nc.sync.dma_start(out=pos3_t[:], in_=pos3)
-        w1_raw = [load_weight(w1, 0, 0)]
-        nc.sync.dma_start(out=w2_raw_w[:].bitcast(I32), in_=w2_words[0].bitcast(I32))
-
-        nc.vector.tensor_copy(v_s_rows[:], tab_s[:].bitcast(U8).indirect(offs_t[:]))
-        place_scale_rows(v_s, v_s_rows)
-        deal_columns(nc.vector.tensor_copy, w2_s_rows[:], w2_raw_s[:].bitcast(U8))
-        place_scale_rows(w2_s, w2_s_rows)
         sc_t = keep.tile([P, GROUPS, PACK], F32, name="w2_raw_s", align_bytes=64)
         nc.sync.dma_start(out=sc_t[:], in_=sc.rearrange("(g p i) -> p g i", p=P, i=PACK))
-        quantize_weight(round_weight(w1_raw[0], -1.0, "w1_first", 1), w1_w, w1_s, 0)
+        quantize(round_weight(w1_early, -1.0, "w1_grouped", 1), w1_w, w1_s, slice(0, PASS))
         deal_columns(nc.scalar.copy, w2_w[:], w2_raw_w[:])
         v_w = []
-        for c in range(S // BANK):
-            tag = "w1_first" if c == S // BANK - 1 else f"v_w{c}"
-            words = ring.tile([P, BANK], U32, name=tag, bufs=1, align_bytes=64)
-            nc.vector.tensor_copy(
-                words[:], tab_w[:].bitcast(U32).indirect(offs_t[:, c * BANK // 16 : (c + 1) * BANK // 16])
+        for c in range(TILES):
+            words = ring.tile(
+                [P, BANK], U32, name="w1_grouped" if c == TILES - 1 else f"v_w{c}", bufs=1, align_bytes=64
             )
+            entries = offs_t[:, c * BANK // PER_COLUMN : (c + 1) * BANK // PER_COLUMN]
+            nc.vector.tensor_copy(words[:], tab_w[:].bitcast(U32).indirect(entries))
             v_w.append(words)
-        w1_raw.append(load_weight(w1, 0, PASS))
+        w1_late = keep.tile([P, PACK, PASS], F32, name="tab_w", align_bytes=64)
+        nc.sync.dma_start(out=w1_late[:], in_=by_word(w1[:, PASS:]))
+        w3_raw = []
+        for g, tag in enumerate(("tab_w", "w2_raw_w")):
+            raw = keep.tile([P, PACK, H], F32, name=tag, align_bytes=64)
+            nc.sync.dma_start(out=raw[:], in_=by_word(w3[g * PASS : (g + 1) * PASS, :]))
+            w3_raw.append(raw)
 
-        h_t, a1_t, tanh_t, sums_t = {}, {}, {}, {}
-        tanh_late = [ring.tile([P, PACK, HALF], F32, name=f"tanh_late{half}", bufs=1, align_bytes=64) for half in range(2)]
+        x_bank, y_bank = ("x_bank", 2), ("y_bank", 3)
+        h_t, x_t, a1_t, tanh_t = {}, {}, {}, {}
+        tanh_late = [ring.tile([P, PACK, HALF], F32, name=f"tanh_late{u}", bufs=1, align_bytes=64) for u in range(2)]
 
-        def products(s):
-            rows = slice(s * P, (s + 1) * P)
-            w1_slice = (w1_w[:, rows].bitcast(FP8X4), w1_s[:, rows])
-            w2_slice = (w2_w[:, rows].bitcast(FP4X4), w2_s[:, rows])
-            h = ring.tile([P, S], F32, name="h", bufs=3)
-            h_t[s] = h
+        def weight_slices(s):
+            places = slice(s * P, (s + 1) * P)
+            return (w1_w[:, places].bitcast(FP8X4), w1_s[:, places]), (w2_w[:, places].bitcast(FP4X4), w2_s[:, places])
 
-            for c in range(TURNED[s]):
-                minus_first = psum.tile([P, PACK, P], F32, name="minus_first")
-                gap = psum.tile([P, PACK, P], F32, name="gap")
-                for bank, weights in ((minus_first, (w1_slice,)), (gap, (w1_slice, w2_slice))):
-                    for block in range(PACK):
-                        cols = slice(c * BANK + block * P, c * BANK + (block + 1) * P)
-                        for n, (words, scales) in enumerate(weights):
-                            nc.tensor.matmul_mx(
-                                out=bank[:, block, :], lhsT=v_w[c][:, block * P : (block + 1) * P].bitcast(FP8X4), lhsT_scale=v_s[:, cols],
-                                rhs=words, rhs_scale=scales, start=(n == 0), stop=(n == len(weights) - 1),
-                            )
-                terms = [ring.tile([P, PACK, P], F32, name=f"term{n}") for n in range(2)]
-                nc.scalar.copy(out=terms[0][:], in_=minus_first[:])
-                nc.scalar.activation(out=terms[1][:], in_=gap[:], func=ACT.Relu, scale=-1.0)
-                turned = psum.tile([P, PACK, P], F32, name="turned")
-                for block in range(PACK):
-                    for n, term in enumerate(terms):
-                        nc.tensor.matmul(
-                            out=turned[:, block, :], lhsT=term[:, block, :], rhs=identity[:],
-                            is_transpose=True, start=(n == 0), stop=(n == 1),
-                        )
-                nc.scalar.activation(
-                    out=h[:, c * BANK : (c + 1) * BANK], in_=turned[:].rearrange("p b j -> p (b j)"), func=ACT.Copy, scale=-1.0
-                )
-
-            sums_t[s] = []
-            for c in range(TURNED[s], S // BANK):
-                cols = slice(c * BANK, (c + 1) * BANK)
-                bank1 = psum.tile([P, BANK], F32, name="bank1", bufs=2)
-                table_product(bank1, w1_slice, cols)
-                first = ring.tile([P, BANK], F32, name="first", bufs=9)
-                nc.scalar.activation(out=first[:], in_=bank1[:], func=ACT.Copy, scale=-1.0)
-                sums_t[s].append((cols, first, w2_slice))
-
-        def table_product(bank, weight, cols):
+        def table_product(tag, weight, c):
+            bank = psum.tile([P, BANK], F32, name=tag[0], bufs=tag[1])
             nc.tensor.matmul_mx(
                 out=bank[:], lhsT=weight[0], lhsT_scale=weight[1],
-                rhs=v_w[cols.start // BANK][:].bitcast(FP8X4), rhs_scale=v_s[:, cols], start=True, stop=True,
+                rhs=v_w[c][:].bitcast(FP8X4), rhs_scale=v_s[:, c * BANK : (c + 1) * BANK], start=True, stop=True,
+            )
+            return bank
+
+        def turned_minimum(s, c):
+            minus_w1, w2_slice = weight_slices(s)
+            terms = ring.tile([P, 2, BANK], F32, name="terms")
+            minus_x = psum.tile([P, BLOCKS, P], F32, name="minus_x")
+            gap = psum.tile([P, BLOCKS, P], F32, name="gap")
+            for bank, weights in ((minus_x, (minus_w1,)), (gap, (minus_w1, w2_slice))):
+                for block in range(BLOCKS):
+                    c0 = block * P
+                    for n, (words, plane) in enumerate(weights):
+                        nc.tensor.matmul_mx(
+                            out=bank[:, block, :], lhsT=v_w[c][:, c0 : c0 + P].bitcast(FP8X4),
+                            lhsT_scale=v_s[:, c * BANK + c0 : c * BANK + c0 + P], rhs=words, rhs_scale=plane,
+                            start=(n == 0), stop=(n == len(weights) - 1),
+                        )
+            nc.scalar.copy(out=terms[:, 0, :], in_=minus_x[:].rearrange("p b r -> p (b r)"))
+            nc.scalar.activation(
+                out=terms[:, 1, :], in_=gap[:].rearrange("p b r -> p (b r)"), func=ACT.Relu, scale=-1.0
+            )
+            turned = psum.tile([P, BLOCKS, P], F32, name="turned")
+            for block in range(BLOCKS):
+                for n in range(2):
+                    nc.tensor.matmul(
+                        out=turned[:, block, :], lhsT=terms[:, n, block * P : (block + 1) * P], rhs=identity[:],
+                        is_transpose=True, start=(n == 0), stop=(n == 1),
+                    )
+            nc.scalar.activation(
+                out=h_t[s][:, c * BANK : (c + 1) * BANK], in_=turned[:].rearrange("p b j -> p (b j)"),
+                func=ACT.Copy, scale=-1.0,
             )
 
+        def prepare(s):
+            h_t[s] = ring.tile([P, S], F32, name="h", bufs=3)
+            for c in range(turned_tiles(s)):
+                turned_minimum(s, c)
+            for c in range(turned_tiles(s), TILES):
+                bank = table_product(x_bank, weight_slices(s)[0], c)
+                x_t[s, c] = ring.tile([P, BANK], F32, name="x", bufs=9)
+                nc.scalar.activation(out=x_t[s, c][:], in_=bank[:], func=ACT.Copy, scale=-1.0)
+
         def minimum(s):
-            for cols, first, w2_slice in sums_t[s]:
-                bank2 = psum.tile([P, BANK], F32, name="bank2", bufs=3)
-                table_product(bank2, w2_slice, cols)
-                nc.vector.tensor_tensor(out=h_t[s][:, cols], in0=bank2[:], in1=first[:], op=ALU.min)
+            for c in range(turned_tiles(s), TILES):
+                bank = table_product(y_bank, weight_slices(s)[1], c)
+                nc.vector.tensor_tensor(
+                    out=h_t[s][:, c * BANK : (c + 1) * BANK], in0=bank[:], in1=x_t[s, c][:], op=ALU.min
+                )
 
         def look_up(s):
             g, i = divmod(s, PACK)
             h = h_t[s]
-            scale = sc_t[:, g, i : i + 1]
             left = ring.tile([P, NP], F32, name="left", bufs=1, align_bytes=64)
             nc.vector.tensor_copy(left[:], h[:].indirect(pos1_t[:]))
             note = ring.tile([P, NK], F32, name="note")
             nc.vector.tensor_copy(note[:], h[:].indirect(pos4_t[:]))
             diff = ring.tile([P, NP], F32, name="diff")
             nc.vector.tensor_tensor(diff[:], h[:].indirect(pos2_t[:]), left[:], ALU.subtract)
-            a1 = ring.tile([P, NP], F32, name="a1", bufs=PACK)
-            nc.scalar.activation(out=a1[:], in_=diff[:], func=ACT.Abs)
-            a1_t[s] = a1
+            a1_t[s] = ring.tile([P, NP], F32, name=f"a1_{i}", bufs=1)
+            nc.scalar.activation(out=a1_t[s][:], in_=diff[:], func=ACT.Abs)
+            scale = sc_t[:, g, i : i + 1]
             if g == 0:
-                tanh_b = ring.tile([P, NK], F32, name="tanh_b")
-                nc.scalar.activation(out=tanh_b[:], in_=note[:], func=ACT.Tanh, scale=scale)
-                tanh_t[s] = tanh_b
+                tanh_t[s] = ring.tile([P, NK], F32, name="tanh_early")
+                nc.scalar.activation(out=tanh_t[s][:], in_=note[:], func=ACT.Tanh, scale=scale)
             else:
-                for half in range(2):
+                for u in range(2):
                     nc.scalar.activation(
-                        out=tanh_late[half][:, i, :], in_=note[:, half * HALF : (half + 1) * HALF], func=ACT.Tanh, scale=scale
+                        out=tanh_late[u][:, i, :], in_=note[:, u * HALF : (u + 1) * HALF], func=ACT.Tanh, scale=scale
                     )
             nc.scalar.activation(out=b_t[g][:, i, :], in_=note[:], func=ACT.Copy, scale=scale)
 
-        def keep_pairs(s, a2, tanh_b, j0, n):
-            nc.vector.tensor_tensor(
-                a2[:, s % PACK, :], a1_t[s][:].indirect(pos3_t[:, j0 // 16 : (j0 + n) // 16]), tanh_b, ALU.mult
+        def keep_pairs(s, a2, tanh_b, cols):
+            entries = pos3_t[:, cols.start // PER_COLUMN : cols.stop // PER_COLUMN]
+            nc.vector.tensor_tensor(a2[:, s % PACK, :], a1_t[s][:].indirect(entries), tanh_b, ALU.mult)
+
+        def quantize_a2(a2, grouped, g, cols):
+            nc.scalar.copy(
+                out=grouped.rearrange("p (c n i) -> p c i n", n=RUN, i=PACK),
+                in_=a2.rearrange("p i (c n) -> p c i n", n=RUN),
             )
+            quantize(grouped, a2_w[g], a2_s[g], cols)
 
-        def round_a2(a2, grouped):
-            nc.scalar.copy(out=grouped.rearrange("p (j i) -> p j i", i=PACK), in_=a2.rearrange("p i j -> p j i"))
+        def quantize_w3(part):
+            g, c0 = part // GROUPS, part % GROUPS * PASS
+            quantize(round_weight(column_halves(w3_raw[g], c0), 1.0), w3_w[g], w3_s[g], slice(c0, c0 + PASS))
 
-        def quantize_a2(grouped, g, j0, n):
-            nc.vector.quantize_mx(
-                out=a2_w[g][:, j0 : j0 + n].bitcast(FP8X4),
-                scales=a2_s[g][:, j0 : j0 + n],
-                in_=grouped,
-            )
-
-        def second_stage(j0, banks):
-            cols = slice(j0, j0 + HALF)
-            for pair in range(SLICES // 2):
-                g, i0 = divmod(2 * pair, PACK)
-                bank = psum.tile([P, 2, HALF], F32, name=banks[pair][0], bufs=banks[pair][1])
-                for kg in range(GROUPS):
-                    for u in range(2):
-                        rows = slice((2 * pair + u) * P, (2 * pair + u + 1) * P)
-                        nc.tensor.matmul_mx(
-                            out=bank[:, u, :], lhsT=w3_w[kg][:, rows].bitcast(FP8X4), lhsT_scale=w3_s[kg][:, rows],
-                            rhs=a2_w[kg][:, cols].bitcast(FP8X4), rhs_scale=a2_s[kg][:, cols],
-                            start=(kg == 0 and u == 0), stop=(kg == GROUPS - 1 and u == 1),
-                        )
-                result = ring.tile([P, 2, HALF], F32, name="result", bufs=4)
-                nc.vector.tensor_tensor(out=result[:], in0=bank[:], in1=b_t[g][:, i0 : i0 + 2, cols], op=ALU.add)
-                nc.sync.dma_start(
-                    out=out[g * PASS : (g + 1) * PASS, cols].rearrange("(p i) j -> p i j", i=PACK)[:, i0 : i0 + 2, :],
-                    in_=result[:],
-                )
-
-        w3_parts = [(kg, c0) for kg in range(GROUPS) for c0 in range(0, H, PASS)]
-        a2_first = keep.tile([P, PACK, NK], F32)
-        products(0)
+        a2_early = keep.tile([P, PACK, NK], F32)
+        prepare(0)
         minimum(0)
-        products(1)
+        prepare(1)
+        quantize(round_weight(column_halves(w1_late, 0), -1.0), w1_w, w1_s, slice(PASS, H))
         for s in range(SLICES):
             if s + 2 < SLICES:
-                products(s + 2)
+                prepare(s + 2)
             look_up(s)
-            if s == 0:
-                quantize_weight(round_weight(w1_raw[1], -1.0), w1_w, w1_s, PASS)
             if s + 1 < SLICES:
                 minimum(s + 1)
             if 1 <= s <= PACK:
-                keep_pairs(s - 1, a2_first, tanh_t[s - 1][:], 0, NK)
-            if 1 <= s < 1 + len(w3_parts):
-                kg, c0 = w3_parts[s - 1]
-                quantize_weight(round_weight(load_weight(w3, kg * PASS, c0), 1.0), w3_w[kg], w3_s[kg], c0)
+                keep_pairs(s - 1, a2_early, tanh_t[s - 1][:], slice(0, NK))
+                quantize_w3(s - 1)
             if s == PACK + 1:
-                grouped = ring.tile([P, NK * PACK], BF16, name="w_grouped", align_bytes=64)
-                round_a2(a2_first[:], grouped[:])
-                quantize_a2(grouped[:], 0, 0, NK)
+                grouped_early = ring.tile([P, NK * PACK], BF16, name="grouped", align_bytes=64)
+                quantize_a2(a2_early[:], grouped_early[:], 0, slice(0, NK))
 
-        a2_halves = [
+        halves = [slice(u * HALF, (u + 1) * HALF) for u in range(2)]
+        tags = [("minus_x", 1), ("gap", 1), ("turned", 1)] + [x_bank] * 2 + [y_bank] * 3
+        pairs = SLICES // 2
+
+        def second_pass(bank, pair, g, cols):
+            for n in range(2):
+                places = slice((2 * pair + n) * P, (2 * pair + n + 1) * P)
+                nc.tensor.matmul_mx(
+                    out=bank[:, n, :], lhsT=w3_w[g][:, places].bitcast(FP8X4), lhsT_scale=w3_s[g][:, places],
+                    rhs=a2_w[g][:, cols].bitcast(FP8X4), rhs_scale=a2_s[g][:, cols],
+                    start=(g == 0 and n == 0), stop=(g == GROUPS - 1 and n == 1),
+                )
+
+        out_banks = []
+        for u, cols in enumerate(halves):
+            banks = [psum.tile([P, 2, HALF], F32, name=tag, bufs=bufs) for tag, bufs in tags[u * pairs : (u + 1) * pairs]]
+            for pair, bank in enumerate(banks):
+                second_pass(bank, pair, 0, cols)
+            out_banks.append(banks)
+
+        a2_late = [
             ring.tile([P, PACK * HALF], F32, name="left", bufs=1, align_bytes=64),
             ring.tile([P, (PACK + 1) * HALF], F32, name="tanh_late0", bufs=1, align_bytes=64),
         ]
-        grouped_last = ring.tile([P, HALF * PACK], BF16, name="w_grouped", align_bytes=64)
-        grouped_halves = [a2_halves[1][:, (PACK - 1) * HALF :].bitcast(BF16), grouped_last[:]]
-        for half in range(2):
-            a2_half = a2_halves[half][:, : PACK * HALF].rearrange("p (i j) -> p i j", i=PACK)
+        grouped_last = ring.tile([P, HALF * PACK], BF16, name="grouped", align_bytes=64)
+        grouped_late = [a2_late[1][:, (PACK - 1) * HALF :].bitcast(BF16), grouped_last[:]]
+        for u, cols in enumerate(halves):
+            a2 = a2_late[u][:, : PACK * HALF].rearrange("p (i j) -> p i j", i=PACK)
             for s in range(PACK, SLICES):
-                keep_pairs(s, a2_half, tanh_late[half][:, s % PACK, :], half * HALF, HALF)
-            round_a2(a2_half, grouped_halves[half])
-            quantize_a2(grouped_halves[half], 1, half * HALF, HALF)
-        second_stage(0, (("minus_first", 1), ("gap", 1), ("turned", 1), ("bank1", 2)))
-        second_stage(HALF, (("bank1", 2), ("bank2", 3), ("bank2", 3), ("bank2", 3)))
+                keep_pairs(s, a2, tanh_late[u][:, s % PACK, :], cols)
+            quantize_a2(a2, grouped_late[u], 1, cols)
+
+        for u, cols in enumerate(halves):
+            for pair, bank in enumerate(out_banks[u]):
+                g, i0 = divmod(2 * pair, PACK)
+                second_pass(bank, pair, 1, cols)
+                result = ring.tile([P, 2, HALF], F32, name="result", bufs=2 * pairs)
+                nc.vector.tensor_tensor(out=result[:], in0=bank[:], in1=b_t[g][:, i0 : i0 + 2, cols], op=ALU.add)
+                rows = out[g * PASS : (g + 1) * PASS, cols].rearrange("(p i) j -> p i j", i=PACK)
+                nc.sync.dma_start(out=rows[:, i0 : i0 + 2, :], in_=result[:])

@@ -82,9 +82,9 @@ def tile_list_inquest_account_contrast_kernel(
 
         def round_weight(halves, sign, tag="grouped", bufs=2):
             grouped = ring.tile([P, PASS * PACK], BF16, name=tag, bufs=bufs, align_bytes=64)
-            dst = grouped[:].rearrange("p (i m j) -> p m i j", i=PACK, j=PACK)
+            dst = grouped[:].rearrange("p (i m j) -> p m j i", i=PACK, j=PACK)
             for half, m0 in zip(halves, range(0, P, P // 2)):
-                src = half.rearrange("p j (m i) -> p m i j", i=PACK)
+                src = half.rearrange("p j (m i) -> p m j i", i=PACK)
                 nc.scalar.activation(out=dst[:, m0 : m0 + P // 2], in_=src, func=ACT.Copy, scale=sign)
             return grouped[:]
 

from contextlib import ExitStack

import concourse.mybir as mybir
from concourse.masks import make_identity

K, T, S, NP, NK, H = 512, 4096, 2048, 1024, 512, 1024
FLOPS = 2 * (2 * K * H * S) + 2 * H * H * NK

F32 = mybir.dt.float32
BF16 = mybir.dt.bfloat16
I32 = mybir.dt.int32
U32 = mybir.dt.uint32
U16 = mybir.dt.uint16
U8 = mybir.dt.uint8
FP8X4 = mybir.dt.float8_e4m3fn_x4
FP4X4 = mybir.dt.float4_e2m1fn_x4
ALU = mybir.AluOpType
ACT = mybir.ActivationFunctionType

P = 128
PACK = 4
PASS = P * PACK
BANK = 512
TILES = S // BANK
BLOCKS = BANK // P
GROUPS = H // PASS
SLICES = H // P
HALF = NK // 2
PER_COLUMN = 16
QUADRANTS, QUADRANT, SCALE_ROWS = 4, 32, 4
ROW0 = P - QUADRANTS * SCALE_ROWS
RUN = 4


def turned_tiles(s):
    return {0: 0, SLICES - 1: 2}.get(s, 1)


def tile_list_inquest_account_contrast_kernel(
    tc, tab_words, tab_scales, offs, pos1, pos2, pos3, pos4, w1, w2_words, w2_scales, w3, sc, out
):
    nc = tc.nc
    with ExitStack() as ctx:
        keep = ctx.enter_context(tc.tile_pool(name="keep", bufs=1))
        ring = ctx.enter_context(tc.tile_pool(name="ring", bufs=2))
        psum = ctx.enter_context(tc.psum_pool(name="psum", bufs=1))

        offs_t = keep.tile([P, S // PER_COLUMN], U16)
        pos1_t = keep.tile([P, NP // PER_COLUMN], U16)
        pos2_t = keep.tile([P, NP // PER_COLUMN], U16)
        pos3_t = keep.tile([P, NK // PER_COLUMN], U16)
        pos4_t = keep.tile([P, NK // PER_COLUMN], U16)
        tab_w = keep.tile([P, T], I32, align_bytes=64)
        tab_s = keep.tile([P, T // 4], I32, align_bytes=64)
        v_s_rows = keep.tile([P, S], U8, align_bytes=64)
        v_s = keep.tile([P, S], U8, align_bytes=64)
        w2_raw_w = keep.tile([P, H], U16, align_bytes=64)
        w2_raw_s = keep.tile([P, H // 4], I32, align_bytes=64)
        w2_w = keep.tile([P, H], U16, align_bytes=64)
        w2_s = keep.tile([P, H], U8, align_bytes=64)
        w1_w = keep.tile([P, H], U32, align_bytes=64)
        w1_s = keep.tile([P, H], U8, align_bytes=64)
        w3_w = [keep.tile([P, H], U32, align_bytes=64, name=f"w3_w{g}") for g in range(GROUPS)]
        w3_s = [keep.tile([P, H], U8, align_bytes=64, name=f"w3_s{g}") for g in range(GROUPS)]
        a2_w = [keep.tile([P, NK], U32, align_bytes=64, name=f"a2_w{g}") for g in range(GROUPS)]
        a2_s = [keep.tile([P, NK], U8, align_bytes=64, name=f"a2_s{g}") for g in range(GROUPS)]
        identity = keep.tile([P, P], F32)
        b_t = [keep.tile([P, PACK, NK], F32, name=f"b{g}") for g in range(GROUPS)]

        def place_scale_rows(plane, rows):
            for q in range(QUADRANTS):
                nc.sync.dma_start(
                    out=plane[QUADRANT * q : QUADRANT * q + SCALE_ROWS, :],
                    in_=rows[SCALE_ROWS * q : SCALE_ROWS * (q + 1), :],
                )

        def by_word(rows):
            return rows.rearrange("(p j) c -> p j c", j=PACK)

        def column_halves(raw, c0):
            return [raw[:, :, c : c + PASS // 2] for c in range(c0, c0 + PASS, PASS // 2)]

        def round_weight(halves, sign, tag="grouped", bufs=2):
            grouped = ring.tile([P, PASS * PACK], BF16, name=tag, bufs=bufs, align_bytes=64)
            dst = grouped[:].rearrange("p (i m j) -> p m j i", i=PACK, j=PACK)
            for half, m0 in zip(halves, range(0, P, P // 2)):
                src = half.rearrange("p j (m i) -> p m j i", i=PACK)
                nc.scalar.activation(out=dst[:, m0 : m0 + P // 2], in_=src, func=ACT.Copy, scale=sign)
            return grouped[:]

        def quantize(grouped, words, plane, cols):
            nc.vector.quantize_mx(out=words[:, cols].bitcast(FP8X4), scales=plane[:, cols], in_=grouped)

        def deal_columns(copy, dst, src):
            copy(
                out=dst.rearrange("p (g i m) -> p g i m", g=GROUPS, i=PACK),
                in_=src.rearrange("p (g m i) -> p g i m", g=GROUPS, i=PACK),
            )

        nc.gpsimd.memset(w2_raw_s[:], 0)
        make_identity(nc, identity[:])
        nc.vector.memset(tab_s[: P - QUADRANT, :], 0)
        nc.vector.memset(tab_s[P - QUADRANT : ROW0, :], 0)
        nc.sync.dma_start(out=offs_t[:], in_=offs)
        nc.sync.dma_start(out=tab_s[ROW0:, :], in_=tab_scales[0].bitcast(I32))
        nc.sync.dma_start(out=tab_w[:], in_=tab_words[0].rearrange("p t i -> p (t i)").bitcast(I32))
        place_scale_rows(w2_raw_s, w2_scales[0].bitcast(I32))
        w1_early = []
        for c in range(0, PASS, PASS // 2):
            raw = ring.tile([P, PACK, PASS // 2], F32, name="w1_early")
            nc.sync.dma_start(out=raw[:], in_=by_word(w1[:, c : c + PASS // 2]))
            w1_early.append(raw[:])
        nc.sync.dma_start(out=w2_raw_w[:].bitcast(I32), in_=w2_words[0].bitcast(I32))

        nc.vector.tensor_copy(v_s_rows[:], tab_s[:].bitcast(U8).indirect(offs_t[:]))
        place_scale_rows(v_s[:].bitcast(I32), v_s_rows[ROW0:, :].bitcast(I32))
        deal_columns(nc.vector.tensor_copy, w2_s[:], w2_raw_s[:].bitcast(U8))
        nc.sync.dma_start(out=pos1_t[:], in_=pos1)
        nc.sync.dma_start(out=pos4_t[:], in_=pos4)
        nc.sync.dma_start(out=pos2_t[:], in_=pos2)
        nc.sync.dma_start(out=pos3_t[:], in_=pos3)
        sc_t = keep.tile([P, GROUPS, PACK], F32, name="w2_raw_s", align_bytes=64)
        nc.sync.dma_start(out=sc_t[:], in_=sc.rearrange("(g p i) -> p g i", p=P, i=PACK))
        quantize(round_weight(w1_early, -1.0, "w1_grouped", 1), w1_w, w1_s, slice(0, PASS))
        deal_columns(nc.scalar.copy, w2_w[:], w2_raw_w[:])
        v_w = []
        for c in range(TILES):
            words = ring.tile(
                [P, BANK], U32, name="w1_grouped" if c == TILES - 1 else f"v_w{c}", bufs=1, align_bytes=64
            )
            entries = offs_t[:, c * BANK // PER_COLUMN : (c + 1) * BANK // PER_COLUMN]
            nc.vector.tensor_copy(words[:], tab_w[:].bitcast(U32).indirect(entries))
            v_w.append(words)
        w1_late = keep.tile([P, PACK, PASS], F32, name="tab_w", align_bytes=64)
        nc.sync.dma_start(out=w1_late[:], in_=by_word(w1[:, PASS:]))
        w3_raw = []
        for g, tag in enumerate(("tab_w", "w2_raw_w")):
            raw = keep.tile([P, PACK, H], F32, name=tag, align_bytes=64)
            nc.sync.dma_start(out=raw[:], in_=by_word(w3[g * PASS : (g + 1) * PASS, :]))
            w3_raw.append(raw)

        x_bank, y_bank = ("x_bank", 2), ("y_bank", 3)
        h_t, x_t, a1_t, tanh_t = {}, {}, {}, {}
        tanh_late = [ring.tile([P, PACK, HALF], F32, name=f"tanh_late{u}", bufs=1, align_bytes=64) for u in range(2)]

        def weight_slices(s):
            places = slice(s * P, (s + 1) * P)
            return (w1_w[:, places].bitcast(FP8X4), w1_s[:, places]), (w2_w[:, places].bitcast(FP4X4), w2_s[:, places])

        def table_product(tag, weight, c):
            bank = psum.tile([P, BANK], F32, name=tag[0], bufs=tag[1])
            nc.tensor.matmul_mx(
                out=bank[:], lhsT=weight[0], lhsT_scale=weight[1],
                rhs=v_w[c][:].bitcast(FP8X4), rhs_scale=v_s[:, c * BANK : (c + 1) * BANK], start=True, stop=True,
            )
            return bank

        def turned_minimum(s, c):
            minus_w1, w2_slice = weight_slices(s)
            terms = ring.tile([P, 2, BANK], F32, name="terms")
            minus_x = psum.tile([P, BLOCKS, P], F32, name="minus_x")
            gap = psum.tile([P, BLOCKS, P], F32, name="gap")
            for bank, weights in ((minus_x, (minus_w1,)), (gap, (minus_w1, w2_slice))):
                for block in range(BLOCKS):
                    c0 = block * P
                    for n, (words, plane) in enumerate(weights):
                        nc.tensor.matmul_mx(
                            out=bank[:, block, :], lhsT=v_w[c][:, c0 : c0 + P].bitcast(FP8X4),
                            lhsT_scale=v_s[:, c * BANK + c0 : c * BANK + c0 + P], rhs=words, rhs_scale=plane,
                            start=(n == 0), stop=(n == len(weights) - 1),
                        )
            nc.scalar.copy(out=terms[:, 0, :], in_=minus_x[:].rearrange("p b r -> p (b r)"))
            nc.scalar.activation(
                out=terms[:, 1, :], in_=gap[:].rearrange("p b r -> p (b r)"), func=ACT.Relu, scale=-1.0
            )
            turned = psum.tile([P, BLOCKS, P], F32, name="turned")
            for block in range(BLOCKS):
                for n in range(2):
                    nc.tensor.matmul(
                        out=turned[:, block, :], lhsT=terms[:, n, block * P : (block + 1) * P], rhs=identity[:],
                        is_transpose=True, start=(n == 0), stop=(n == 1),
                    )
            nc.scalar.activation(
                out=h_t[s][:, c * BANK : (c + 1) * BANK], in_=turned[:].rearrange("p b j -> p (b j)"),
                func=ACT.Copy, scale=-1.0,
            )

        def prepare(s):
            h_t[s] = ring.tile([P, S], F32, name="h", bufs=3)
            for c in range(turned_tiles(s)):
                turned_minimum(s, c)
            for c in range(turned_tiles(s), TILES):
                bank = table_product(x_bank, weight_slices(s)[0], c)
                x_t[s, c] = ring.tile([P, BANK], F32, name="x", bufs=9)
                nc.scalar.activation(out=x_t[s, c][:], in_=bank[:], func=ACT.Copy, scale=-1.0)

        def minimum(s):
            for c in range(turned_tiles(s), TILES):
                bank = table_product(y_bank, weight_slices(s)[1], c)
                nc.vector.tensor_tensor(
                    out=h_t[s][:, c * BANK : (c + 1) * BANK], in0=bank[:], in1=x_t[s, c][:], op=ALU.min
                )

        def look_up(s):
            g, i = divmod(s, PACK)
            h = h_t[s]
            left = ring.tile([P, NP], F32, name="left", bufs=1, align_bytes=64)
            nc.vector.tensor_copy(left[:], h[:].indirect(pos1_t[:]))
            note = ring.tile([P, NK], F32, name="note")
            nc.vector.tensor_copy(note[:], h[:].indirect(pos4_t[:]))
            diff = ring.tile([P, NP], F32, name="diff")
            nc.vector.tensor_tensor(diff[:], h[:].indirect(pos2_t[:]), left[:], ALU.subtract)
            a1_t[s] = ring.tile([P, NP], F32, name=f"a1_{i}", bufs=1)
            nc.scalar.activation(out=a1_t[s][:], in_=diff[:], func=ACT.Abs)
            scale = sc_t[:, g, i : i + 1]
            if g == 0:
                tanh_t[s] = ring.tile([P, NK], F32, name="tanh_early")
                nc.scalar.activation(out=tanh_t[s][:], in_=note[:], func=ACT.Tanh, scale=scale)
            else:
                for u in range(2):
                    nc.scalar.activation(
                        out=tanh_late[u][:, i, :], in_=note[:, u * HALF : (u + 1) * HALF], func=ACT.Tanh, scale=scale
                    )
            nc.scalar.activation(out=b_t[g][:, i, :], in_=note[:], func=ACT.Copy, scale=scale)

        def keep_pairs(s, a2, tanh_b, cols):
            entries = pos3_t[:, cols.start // PER_COLUMN : cols.stop // PER_COLUMN]
            nc.vector.tensor_tensor(a2[:, s % PACK, :], a1_t[s][:].indirect(entries), tanh_b, ALU.mult)

        def quantize_a2(a2, grouped, g, cols):
            nc.scalar.copy(
                out=grouped.rearrange("p (c n i) -> p c i n", n=RUN, i=PACK),
                in_=a2.rearrange("p i (c n) -> p c i n", n=RUN),
            )
            quantize(grouped, a2_w[g], a2_s[g], cols)

        def quantize_w3(part):
            g, c0 = part // GROUPS, part % GROUPS * PASS
            quantize(round_weight(column_halves(w3_raw[g], c0), 1.0), w3_w[g], w3_s[g], slice(c0, c0 + PASS))

        a2_early = keep.tile([P, PACK, NK], F32)
        prepare(0)
        minimum(0)
        prepare(1)
        quantize(round_weight(column_halves(w1_late, 0), -1.0), w1_w, w1_s, slice(PASS, H))
        for s in range(SLICES):
            if s + 2 < SLICES:
                prepare(s + 2)
            look_up(s)
            if s + 1 < SLICES:
                minimum(s + 1)
            if 1 <= s <= PACK:
                keep_pairs(s - 1, a2_early, tanh_t[s - 1][:], slice(0, NK))
                quantize_w3(s - 1)
            if s == PACK + 1:
                grouped_early = ring.tile([P, NK * PACK], BF16, name="grouped", align_bytes=64)
                quantize_a2(a2_early[:], grouped_early[:], 0, slice(0, NK))

        halves = [slice(u * HALF, (u + 1) * HALF) for u in range(2)]
        tags = [("minus_x", 1), ("gap", 1), ("turned", 1)] + [x_bank] * 2 + [y_bank] * 3
        pairs = SLICES // 2

        def second_pass(bank, pair, g, cols):
            for n in range(2):
                places = slice((2 * pair + n) * P, (2 * pair + n + 1) * P)
                nc.tensor.matmul_mx(
                    out=bank[:, n, :], lhsT=w3_w[g][:, places].bitcast(FP8X4), lhsT_scale=w3_s[g][:, places],
                    rhs=a2_w[g][:, cols].bitcast(FP8X4), rhs_scale=a2_s[g][:, cols],
                    start=(g == 0 and n == 0), stop=(g == GROUPS - 1 and n == 1),
                )

        out_banks = []
        for u, cols in enumerate(halves):
            banks = [psum.tile([P, 2, HALF], F32, name=tag, bufs=bufs) for tag, bufs in tags[u * pairs : (u + 1) * pairs]]
            for pair, bank in enumerate(banks):
                second_pass(bank, pair, 0, cols)
            out_banks.append(banks)

        a2_late = [
            ring.tile([P, PACK * HALF], F32, name="left", bufs=1, align_bytes=64),
            ring.tile([P, (PACK + 1) * HALF], F32, name="tanh_late0", bufs=1, align_bytes=64),
        ]
        grouped_last = ring.tile([P, HALF * PACK], BF16, name="grouped", align_bytes=64)
        grouped_late = [a2_late[1][:, (PACK - 1) * HALF :].bitcast(BF16), grouped_last[:]]
        for u, cols in enumerate(halves):
            a2 = a2_late[u][:, : PACK * HALF].rearrange("p (i j) -> p i j", i=PACK)
            for s in range(PACK, SLICES):
                keep_pairs(s, a2, tanh_late[u][:, s % PACK, :], cols)
            quantize_a2(a2, grouped_late[u], 1, cols)

        for u, cols in enumerate(halves):
            for pair, bank in enumerate(out_banks[u]):
                g, i0 = divmod(2 * pair, PACK)
                second_pass(bank, pair, 1, cols)
                result = ring.tile([P, 2, HALF], F32, name="result", bufs=2 * pairs)
                nc.vector.tensor_tensor(out=result[:], in0=bank[:], in1=b_t[g][:, i0 : i0 + 2, cols], op=ALU.add)
                rows = out[g * PASS : (g + 1) * PASS, cols].rearrange("(p i) j -> p i j", i=PACK)
                nc.sync.dma_start(out=rows[:, i0 : i0 + 2, :], in_=result[:])
